import numpy as np, ml_dtypes
CORES = [23,119,17,113]
N = 4
import mx_ref
NC, GR, GC, KT = 128, 2, 2, 1
TS = GC * KT
CH = GR * NC // GC
BF = ml_dtypes.bfloat16
def setup_inputs(rng):
    def f(*shape):
        return mx_ref.flush((rng.standard_normal(shape, dtype=np.float32) * np.exp2(rng.integers(-2, 3, shape[:-1] + (1,)))).astype(BF))
    return {"w": f(N, 128, KT * 512), "x": f(N, 128, KT * 4 * NC)}
def setup_inputs_blocks(rng):
    d = setup_inputs(rng)
    for k in ("w", "x"): d[k] = mx_ref.spread(d[k], rng, 1)
    return d
def setup_inputs_wide(rng):
    d = setup_inputs(rng)
    for k in ("w", "x"): d[k] = mx_ref.flush((d[k].astype(np.float32) * np.exp2(rng.integers(-8, 9, (N, 1, 1))).astype(np.float32)).astype(BF))
    return d
def setup_inputs_zeros(rng):
    d = setup_inputs(rng); v = d["x"].reshape(N, 128, -1, 4).copy()
    v[np.broadcast_to((rng.random((N, 1, v.shape[2], 1)) < 0.33), v.shape)] = 0
    d["x"] = v.reshape(d["x"].shape)
    return d
def reference(w, x):
    QX = [[mx_ref.quantize(x[r][:, 4 * NC * t:4 * NC * t + 4 * NC]) for t in range(KT)] for r in range(N)]
    y = np.zeros((N, 128, CH), np.float32)
    for i in range(GR):
        for s in range(TS):
            k, t = s // KT, s % KT
            qw = mx_ref.quantize(w[i * GC + k][:, 512 * t:512 * t + 512])
            p = np.concatenate([mx_ref.matmul(qw, QX[g * GC + k][t]) for g in range(GR)], axis=1)
            Y = p if s == 0 else Y + p
        for c in range(GC):
            y[i * GC + c] = Y[:, CH * c:CH * c + CH]
    return {"y": y}

from concourse.mybir import dt, AluOpType

GC = 2
NC = 128

SCRATCH = {
    "xb": ("sbuf", [128, 4 * NC], "bfloat16"),
    "wb": ("sbuf", [128, 512], "bfloat16"),
    "xq": ("sbuf", [128, NC], "float8_e4m3fn_x4"),
    "xs": ("sbuf", [128, NC], "uint8"),
    "wq": ("sbuf", [128, 128], "float8_e4m3fn_x4"),
    "ws": ("sbuf", [128, 128], "uint8"),
    "mq": ("sbuf", [128, NC], "float8_e4m3fn_x4"),
    "ms": ("sbuf", [128, NC], "uint8"),
    "keep": ("psum", [128, 512], "float32"),
    "give": ("psum", [128, 512], "float32"),
    "part": ("sbuf", [128, NC], "float32"),
    "land": ("sbuf", [128, NC], "float32"),
    "out": ("sbuf", [128, NC], "float32"),
}
SEMAPHORES = ["ldx", "ldw", "qx", "qw", "xarr", "mml", "mmr", "cp", "parr", "added", "stored", "sent"]


def _engines(mask):
    return [1 << e for e in range(mask.bit_length()) if (mask >> e) & 1]


def rank_program(g, core, T, topo):
    rank = T.rank_of(core)
    if rank is None:
        return
    S = T.sem
    row, col = divmod(rank, GC)
    col_mate = T.cores[(1 - row) * GC + col]
    row_mate = T.cores[row * GC + (1 - col)]
    for dst in (col_mate, row_mate):
        if not topo.may_write(core, dst):
            raise ValueError("core %d may not write to core %d" % (core, dst))
    local_is_kept = row == col
    acc_local, acc_mate = (T.keep, T.give) if local_is_kept else (T.give, T.keep)
    sem_keep, sem_give = (S.mml, S.mmr) if local_is_kept else (S.mmr, S.mml)

    x_eng = _engines(topo.mask(core, col_mate))
    codes_mask, plane_mask = sum(x_eng[0::2]), sum(x_eng[1::2])
    n_codes, n_plane = len(x_eng[0::2]), len(x_eng[1::2])
    part_mask = topo.mask(core, row_mate)
    n_part = len(_engines(part_mask))

    g.sync.dma_start(T.xb[:], T.x[:]).then_inc(S.ldx, 16)
    g.sync.dma_start(T.wb[:], T.w[:]).then_inc(S.ldw, 16)

    g.vector.wait_ge(S.ldx, 16)
    g.vector.quantize_mx(T.xq[:], T.xs[:], T.xb[:]).then_inc(S.qx, 1)
    g.vector.wait_ge(S.ldw, 16)
    g.vector.quantize_mx(T.wq[:], T.ws[:], T.wb[:]).then_inc(S.qw, 1)

    rid, pid, _ = topo.addr(col_mate)
    g.wait_ge(S.qx, 1)
    g.remote_dma(out_ap=T.mq[:].bitcast(dt.uint8), in_ap=T.xq[:].bitcast(dt.uint8), remote_sem=S.xarr,
                 local_sem=S.sent, pid=pid, routing_id=rid, dma_engine_mask=codes_mask)
    g.remote_dma(out_ap=T.ms[:], in_ap=T.xs[:], remote_sem=S.xarr,
                 local_sem=S.sent, pid=pid, routing_id=rid, dma_engine_mask=plane_mask)

    g.tensor.wait_ge(S.qx, 1)
    g.tensor.wait_ge(S.qw, 1)
    g.tensor.matmul_mx(acc_local[:, 0:NC], T.wq[:], T.ws[:], T.xq[:], T.xs[:], True, True).then_inc(S.mml, 1)
    g.tensor.wait_ge(S.xarr, n_codes + n_plane)
    g.tensor.matmul_mx(acc_mate[:, 0:NC], T.wq[:], T.ws[:], T.mq[:], T.ms[:], True, True).then_inc(S.mmr, 1)

    g.vector.wait_ge(sem_give, 1)
    g.vector.tensor_copy(T.part[:], T.give[:, 0:NC]).then_inc(S.cp, 1)

    rid, pid, _ = topo.addr(row_mate)
    g.wait_ge(S.cp, 1)
    g.remote_dma(out_ap=T.land[:], in_ap=T.part[:], remote_sem=S.parr,
                 local_sem=S.sent, pid=pid, routing_id=rid, dma_engine_mask=part_mask)

    g.vector.wait_ge(sem_keep, 1)
    g.vector.wait_ge(S.parr, n_part)
    g.vector.tensor_tensor(T.out[:], T.keep[:, 0:NC], T.land[:], AluOpType.add).then_inc(S.added, 1)

    g.sync.wait_ge(S.added, 1)
    g.sync.dma_start(T.y[:], T.out[:]).then_inc(S.stored, 16)
    g.sync.wait_ge(S.stored, 16)

    g.wait_ge(S.sent, n_codes + n_plane + n_part)
